import numpy as np
import ml_dtypes


def mxq(x, axis, fmt="e4m3"):
    dtype, down = {"e4m3": (ml_dtypes.float8_e4m3fn, 7), "e5m2": (ml_dtypes.float8_e5m2, 14)}[fmt]
    v = np.moveaxis(np.asarray(x, np.float32).astype(ml_dtypes.bfloat16).astype(np.float64), axis, -1)
    blocks = v.reshape(v.shape[:-1] + (-1, 32))
    amax = np.abs(blocks).max(-1, keepdims=True)
    byte = np.maximum(np.where(amax > 0, np.frexp(amax)[1] - 1 + 127, 0) - down, 1)
    scale = np.exp2(byte - 127.0)
    codes = (blocks / scale).astype(np.float32).astype(dtype).astype(np.float64)
    return np.moveaxis((codes * scale).reshape(v.shape), -1, axis)


WIDE = False


def mx_kscale(k):
    if not WIDE:
        return np.ones(k)
    levels = np.array([10, -10, 5, -5, 0])
    if k % 512:
        return np.exp2(np.random.permutation(np.resize(levels, k // 32))).repeat(32)
    a = np.empty((k // 512, 16))
    for p in range(k // 512):
        a[p, :8] = np.random.permutation(np.resize(levels, 8))
        for g in range(8):
            far = levels[np.abs(levels - a[p, g]) >= 10]
            a[p, g + 8] = far[np.random.randint(len(far))]
    return np.exp2(a.ravel()).repeat(32)


def f64(x):
    return np.asarray(x).astype(np.float64)


def striped(idx):
    return np.tile(np.asarray(idx).reshape(-1, 16).T, (8, 1)).astype(np.uint16)


def unstriped(offs):
    return offs[:16].T.reshape(-1).astype(np.int64)


E2M1 = np.array([0.0, 0.5, 1.0, 1.5, 2.0, 3.0, 4.0, 6.0, -0.0, -0.5, -1.0, -1.5, -2.0, -3.0, -4.0, -6.0])


def pack_weight(w, fmt):
    k, n = w.shape
    w = f64(np.asarray(w, np.float32).astype(ml_dtypes.bfloat16)).reshape(k // 32, 32, n)
    amax = np.abs(w).max(1)
    if fmt == "e4m3":
        byte = np.frexp(amax)[1] - 1 + 127 - 7
    else:
        mant, ex = np.frexp(amax / 6.0)
        byte = np.where(mant > 0.5, ex, ex - 1) + 127
    byte = np.clip(np.where(amax > 0, byte, 1), 1, 254)
    scaled = (w * np.exp2(127.0 - byte)[:, None, :]).reshape(k, n).astype(np.float32)
    by_word = np.ascontiguousarray(scaled.reshape(k // 512, 128, 4, n).transpose(0, 1, 3, 2))
    if fmt == "e4m3":
        words = by_word.astype(ml_dtypes.float8_e4m3fn).view(np.uint8)
    else:
        c = by_word.astype(ml_dtypes.float4_e2m1fn).view(np.uint8) & 0xF
        words = (c[..., 0::2] | (c[..., 1::2] << 4)).reshape(k // 512, 128, 2 * n)
    return np.ascontiguousarray(words), np.ascontiguousarray(byte.astype(np.uint8).reshape(k // 512, 16, n))


def unpack_weight(words, scales, fmt):
    g, _, n = scales.shape
    words = np.ascontiguousarray(words).reshape(g, 128, n, -1)
    if fmt == "e4m3":
        vals = words.view(ml_dtypes.float8_e4m3fn).astype(np.float64)
    else:
        nib = np.empty((g, 128, n, 4), np.uint8)
        nib[..., 0::2] = words & 0xF
        nib[..., 1::2] = words >> 4
        vals = E2M1[nib]
    vals = vals * np.repeat(np.exp2(scales.astype(np.float64) - 127.0), 8, axis=1)[..., None]
    return vals.transpose(0, 1, 3, 2).reshape(g * 512, n)


D, K, R, T, I, Q, G = 512, 512, 512, 2048, 512, 128, 64


def setup_inputs():
    n = np.random.standard_normal
    idx = np.random.permutation(T)[:I]
    fd = mx_kscale(D)
    fk = mx_kscale(K)
    fi = mx_kscale(I)
    keysp = pack_weight(n((D, T)) / fd[:, None], "e4m3")
    tabp = pack_weight(n((K, T)) / fk[:, None], "e4m3")
    return {
        "query": (n((D, Q)) * 0.6 / np.sqrt(D) * fd[:, None]).astype(np.float32),
        "keys_words": keysp[0],
        "keys_scales": keysp[1],
        "sharp": (np.random.uniform(1.0, 3.0, (Q, 1))).astype(np.float32),
        "tab_words": tabp[0],
        "tab_scales": tabp[1],
        "w1": (n((K, R)) * 1 / np.sqrt(K) * fk[:, None]).astype(np.float32),
        "gain": (np.random.uniform(0.5, 2.0, (R, 1))).astype(np.float32),
        "os": (np.random.uniform(4.0, 16.0, (1, I)) * fi).astype(np.float32),
        "vs": (np.random.uniform(0.5, 2.0, (1, I)) / fi).astype(np.float32),
        "offs": striped(idx),
    }


def reference(query, keys_words, keys_scales, sharp, tab_words, tab_scales, w1, gain, os, vs, offs):
    idx = unstriped(offs)
    keysu = unpack_weight(keys_words, keys_scales, "e4m3")
    tabu = unpack_weight(tab_words, tab_scales, "e4m3")
    queryq = mxq(f64(query), 0, "e4m3")
    keysidxg = keysu[:, idx]
    a = queryq.T @ keysidxg
    p = np.exp(a)
    s = p.reshape(Q, G, I // G).sum(axis=2)
    ms = a.reshape(Q, G, I // G).mean(axis=2) * f64(sharp)
    pg = np.exp(ms - np.max(ms, axis=1, keepdims=True))
    z = np.sum(pg, axis=1, keepdims=True)
    sh = pg / z / s
    rr = np.repeat(sh, I // G, axis=1)
    w = p * rr
    w1q = mxq(f64(w1), 0, "e4m3")
    tabidxg = tabu[:, idx]
    zh = w1q.T @ tabidxg
    ht = np.tanh(zh)
    hv = ht * f64(gain)
    wo1 = w * f64(os)
    wt1 = wo1.T
    hw = hv * f64(vs)
    ht1 = hw.T
    wt1q = mxq(wt1, 0, "e4m3")
    ht1q = mxq(ht1, 0, "e4m3")
    o = wt1q.T @ ht1q
    return o

@@ -1,0 +1,272 @@
+from contextlib import ExitStack
+
+import concourse.mybir as mybir
+
+F32 = mybir.dt.float32
+BF16 = mybir.dt.bfloat16
+I32 = mybir.dt.int32
+U32 = mybir.dt.uint32
+U16 = mybir.dt.uint16
+U8 = mybir.dt.uint8
+FP8X4 = mybir.dt.float8_e4m3fn_x4
+ALU = mybir.AluOpType
+ACT = mybir.ActivationFunctionType
+AXIS = mybir.AxisListType
+
+P = 128
+PACK = 4
+TOKENS = 2048
+SLOTS = 512
+HIDDEN = 512
+QUERIES = 128
+GROUP = 8
+GROUPS = SLOTS // GROUP
+CHUNK = 128
+CHUNKS = HIDDEN // CHUNK
+FLOPS = 2 * 512 * QUERIES * SLOTS + 2 * 512 * HIDDEN * SLOTS + 2 * SLOTS * QUERIES * HIDDEN
+
+
+def tile_attend_lrgained_bygroup_kernel(tc, query, keys_words, keys_scales, sharp, tab_words, tab_scales, w1, gain, slot_factor, slot_scale, offs, out):
+    nc = tc.nc
+    with ExitStack() as ctx:
+        lists = ctx.enter_context(tc.tile_pool(name="lists", bufs=1))
+        sb = ctx.enter_context(tc.tile_pool(name="sb", bufs=1))
+        ps = ctx.enter_context(tc.psum_pool(name="ps", bufs=1))
+
+        def tile(name, shape, dtype, tag=""):
+            return sb.tile(shape, dtype, name=name, tag=tag, align_bytes=64)
+
+        def bank(index):
+            return ps.tile([P, PACK, P], F32, name="bank%d" % index)
+
+        def interleave(copy, dst, src):
+            copy(dst.rearrange("p (c i) j -> p c j i", i=4), src.rearrange("p j (c i) -> p c j i", i=4))
+
+        def quantise(name, grouped, width, tag=""):
+            codes = tile(name + "_codes", [P, width], U32, tag)
+            scales = tile(name + "_scales", [P, width], U8)
+            nc.vector.quantize_mx(out=codes[:].bitcast(FP8X4), scales=scales[:], in_=grouped.rearrange("p c j -> p (c j)"))
+            return codes, scales
+
+        def load_scale_rows(queue, plane, source):
+            for quad in range(4):
+                queue.dma_start(plane[32 * quad : 32 * quad + 4, :].bitcast(I32), source[0, 4 * quad : 4 * quad + 4, :].bitcast(I32))
+
+        offsets = lists.tile([P, SLOTS // 16], U16, name="offsets")
+        key_plane = tile("key_plane", [P, TOKENS], U8)
+        nc.vector.memset(key_plane[:].bitcast(I32), 0)
+        gain_cols = tile("gain_cols", [P, PACK], F32, "d")
+        vs_cols = tile("vs_cols", [P, PACK], F32)
+        key_pool = tile("key_pool", [P, TOKENS], U32, "k")
+        query_raw = tile("query_raw", [P, PACK, QUERIES], F32)
+        nc.sync.dma_start(offsets[:], offs)
+        nc.scalar.dma_start(gain_cols[:], gain.rearrange("(n c) o -> n (c o)", c=PACK))
+        nc.sync.dma_start(query_raw[:], query.rearrange("(p j) q -> p j q", j=PACK))
+        nc.scalar.dma_start(vs_cols[:], slot_scale.rearrange("o (p t) -> (o p) t", t=PACK))
+        nc.sync.dma_start(key_pool[:].bitcast(I32), keys_words[0].rearrange("p n t -> p (n t)").bitcast(I32))
+        load_scale_rows(nc.scalar, key_plane, keys_scales)
+
+        identity = tile("identity", [P, P], F32)
+        ones = tile("ones", [P, P], F32, "a")
+        steps = tile("steps", [P, P], F32, "e")
+        ramp = tile("ramp", [P, P], F32, "c")
+        in_quad = tile("in_quad", [P, 32], F32, "f")
+        quad_base = tile("quad_base", [P, 1], F32, "b")
+        warm = tile("warm", [P, 8], F32)
+        nc.vector.memset(ones[:], 1.0)
+        nc.vector.memset(steps[:], 1.0)
+        nc.vector.memset(warm[:], 0.0)
+        for quad in range(4):
+            nc.vector.memset(quad_base[32 * quad : 32 * quad + 32, :], 32.0 * quad)
+        nc.vector.tensor_tensor_scan(ramp[:], ones[:], steps[:], -1.0, ALU.mult, ALU.add)
+        nc.vector.transpose(in_quad[:], ramp[:, 0:32])
+        nc.vector.tensor_scalar(identity[:], ramp[:], quad_base[:], in_quad[:, 0:1], ALU.subtract, ALU.is_equal)
+        warm_out = tile("warm_out", [P, 8], F32)
+        nc.scalar.activation(warm_out[:], warm[:], ACT.Exp)
+
+        def load_w1(u, tag):
+            raw = tile("w1_raw%d" % u, [P, PACK, 2 * CHUNK], F32, tag)
+            nc.sync.dma_start(raw[:], w1[:, u * 2 * CHUNK : (u + 1) * 2 * CHUNK].rearrange("(p j) r -> p j r", j=PACK))
+            return raw
+
+        sharp_col = tile("sharp_col", [P, 1], F32, "a")
+        tab_pool = tile("tab_pool", [P, TOKENS], U32, "e")
+        os_cols = tile("os_cols", [P, PACK], F32, "b")
+        tab_plane = tile("tab_plane", [P, TOKENS], U8, "c")
+        nc.vector.memset(tab_plane[:].bitcast(I32), 0)
+        nc.sync.dma_start(sharp_col[:], sharp)
+        nc.sync.dma_start(tab_pool[:].bitcast(I32), tab_words[0].rearrange("p n t -> p (n t)").bitcast(I32))
+        nc.sync.dma_start(os_cols[:], slot_factor.rearrange("o (p t) -> (o p) t", t=PACK))
+        w1_raw = [load_w1(0, "f")]
+        load_scale_rows(nc.scalar, tab_plane, tab_scales)
+
+        gain_rows = bank(0)
+        for c in range(PACK):
+            nc.tensor.transpose(gain_rows[:, c, :], gain_cols[:, c : c + 1].to_broadcast([P, P]), identity[:])
+        w1_raw.append(load_w1(1, "d"))
+        factor = tile("factor", [P, PACK, HIDDEN], F32)
+        for t in range(PACK):
+            nc.scalar.activation(
+                factor[:, t, :].rearrange("p (n c) -> p n c", c=PACK),
+                gain_rows[:].rearrange("p c n -> p n c"),
+                ACT.Copy,
+                scale=vs_cols[:, t : t + 1],
+            )
+
+        query_grouped = tile("query_grouped", [P, QUERIES, PACK], BF16)
+        interleave(nc.vector.tensor_copy, query_grouped[:], query_raw[:])
+        query_codes, query_scales = quantise("query", query_grouped[:], QUERIES)
+
+        key_scales = tile("key_scales", [P, SLOTS], U8)
+        key_words = tile("key_words", [P, SLOTS], U32)
+        nc.vector.tensor_copy(key_scales[:], key_plane[:].indirect(offsets[:]))
+        nc.vector.tensor_copy(key_words[:], key_pool[:].indirect(offsets[:]))
+        tab_scales_listed = tile("tab_scales_listed", [P, SLOTS], U8, "k")
+        nc.vector.tensor_copy(tab_scales_listed[:], tab_plane[:].indirect(offsets[:]))
+        tab_dealt = tile("tab_dealt", [P, SLOTS], U32)
+        nc.vector.tensor_copy(tab_dealt[:].rearrange("p (t s) -> p s t", t=PACK), tab_pool[:].indirect(offsets[:]))
+        tab_scales_dealt = tile("tab_scales_dealt", [P, SLOTS], U8)
+        nc.vector.tensor_copy(
+            tab_scales_dealt[:].rearrange("p (t s) -> p t s", t=PACK),
+            tab_scales_listed[:].rearrange("p (s t) -> p t s", t=PACK),
+        )
+
+        neg_sharp = tile("neg_sharp", [P, 1], F32)
+        nc.scalar.mul(neg_sharp[:], sharp_col[:], -1.0 / GROUP)
+
+        scores = ps.tile([P, SLOTS], F32, name="bank1")
+        nc.tensor.matmul_mx(
+            out=scores[:],
+            lhsT=query_codes[:].bitcast(FP8X4),
+            lhsT_scale=query_scales[:],
+            rhs=key_words[:].bitcast(FP8X4),
+            rhs_scale=key_scales[:],
+            start=True,
+            stop=True,
+        )
+        both = tile("both", [P, PACK, 2 * P], F32)
+        nc.scalar.activation(both[:, :, 0:P], scores[:].rearrange("q (s t) -> q t s", t=PACK), ACT.Exp)
+        nc.scalar.copy(both[:, :, P : 2 * P], scores[:].rearrange("q (s t) -> q t s", t=PACK))
+
+        probs_turned = bank(2)
+        for t in range(PACK):
+            nc.tensor.transpose(probs_turned[:, t, :], both[:, t, 0:P], identity[:])
+        sums_turned = ps.tile([P, QUERIES], F32, name="bank3")
+        for j in range(GROUP):
+            nc.tensor.matmul(
+                sums_turned[:], both[:, j // 2, j % 2 : 2 * P : 2], identity[:], start=(j == 0), stop=(j == GROUP - 1), is_transpose=True
+            )
+        weighted = tile("weighted", [P, PACK, QUERIES], F32, "h")
+        for t in range(PACK):
+            nc.scalar.activation(weighted[:, t, :], probs_turned[:, t, :], ACT.Copy, scale=os_cols[:, t : t + 1])
+        sums_staged = tile("sums_staged", [P, QUERIES], F32)
+        nc.scalar.copy(sums_staged[:], sums_turned[:])
+        sums = ps.tile([P, 2 * GROUPS], F32, name="bank4")
+        nc.tensor.transpose(sums[:], sums_staged[:], identity[:])
+
+        w1_quantised = []
+
+        def prepare_w1(u):
+            grouped = tile("w1_grouped%d" % u, [P, 2 * CHUNK, PACK], BF16, "g%d" % u)
+            for c in range(2):
+                cols = slice(c * CHUNK, (c + 1) * CHUNK)
+                copy = nc.vector.tensor_copy if (u, c) == (0, 0) else nc.scalar.copy
+                interleave(copy, grouped[:, cols, :], w1_raw[u][:, :, cols])
+            w1_quantised.append(quantise("w1_%d" % u, grouped[:], 2 * CHUNK, "e" if u == 0 else ""))
+
+        layer_banks = [6, 7, 0, 1]
+        out_banks = [2, 3, 4, 5]
+        tanhs = []
+
+        def layer_chunk(c):
+            layer = bank(layer_banks[c])
+            codes, scales = w1_quantised[c // 2]
+            cols = slice((c % 2) * CHUNK, (c % 2 + 1) * CHUNK)
+            for t in range(PACK):
+                slots = slice(t * P, (t + 1) * P)
+                nc.tensor.matmul_mx(
+                    out=layer[:, t, :],
+                    lhsT=tab_dealt[:, slots].bitcast(FP8X4),
+                    lhsT_scale=tab_scales_dealt[:, slots],
+                    rhs=codes[:, cols].bitcast(FP8X4),
+                    rhs_scale=scales[:, cols],
+                    start=True,
+                    stop=True,
+                )
+            squashed = tile("squashed%d" % c, [P, CHUNK, PACK], F32)
+            nc.scalar.activation(squashed[:], layer[:].rearrange("p t r -> p r t"), ACT.Tanh)
+            tanhs.append(squashed)
+
+        prepare_w1(0)
+        stats = tile("stats", [P, 2, GROUPS], F32, "g0")
+        neg_means = stats[:, 0, :]
+        inv_sums = stats[:, 1, :]
+        neg_max = tile("neg_max", [P, 1], F32)
+        nc.vector.tensor_scalar(neg_means, sums[:, GROUPS : 2 * GROUPS], neg_sharp[:], None, ALU.mult, ALU.min, accum_out=neg_max[:])
+        nc.vector.reciprocal(inv_sums, sums[:, 0:GROUPS])
+        group_probs = tile("group_probs", [P, GROUPS], F32)
+        group_total = tile("group_total", [P, 1], F32)
+        nc.scalar.activation(group_probs[:], neg_means, ACT.Exp, bias=neg_max[:], scale=-1.0, accum_out=group_total[:])
+
+        prepare_w1(1)
+        layer_chunk(0)
+
+        inv_total = tile("inv_total", [P, 1], F32)
+        nc.vector.reciprocal(inv_total[:], group_total[:])
+        shares = tile("shares", [P, GROUPS, 2], F32)
+        nc.vector.scalar_tensor_tensor(
+            shares[:],
+            group_probs[:].unsqueeze(2).to_broadcast([P, GROUPS, 2]),
+            inv_total[:],
+            inv_sums.unsqueeze(2).to_broadcast([P, GROUPS, 2]),
+            ALU.mult,
+            ALU.mult,
+        )
+        shares_turned = ps.tile([P, QUERIES], F32, name="bank6")
+        nc.tensor.transpose(shares_turned[:], shares[:].rearrange("q g h -> q (g h)"), identity[:])
+
+        for c in range(1, CHUNKS):
+            layer_chunk(c)
+
+        weights = tile("weights", [P, QUERIES, PACK], BF16, "i")
+        nc.vector.tensor_tensor(
+            weights[:],
+            weighted[:].rearrange("p t q -> p q t"),
+            shares_turned[:].unsqueeze(2).to_broadcast([P, QUERIES, PACK]),
+            ALU.mult,
+        )
+        weight_codes, weight_scales = quantise("weights", weights[:], QUERIES)
+
+        first = tile("first", [P, 3 * CHUNK], F32)
+        last = tile("last", [P, CHUNK], F32)
+        scaled = []
+
+        def scale_chunk(c):
+            values = tile("values%d" % c, [P, CHUNK, PACK], BF16, {2: "h", 3: "i"}.get(c, ""))
+            nc.vector.tensor_tensor(
+                values[:], tanhs[c][:], factor[:, :, c * CHUNK : (c + 1) * CHUNK].rearrange("p t r -> p r t"), ALU.mult
+            )
+            scaled.append(values)
+
+        def finish_chunk(c):
+            codes, scales = quantise("values%d" % c, scaled[c][:], CHUNK)
+            result = ps.tile([P, CHUNK], F32, name="bank%d" % out_banks[c])
+            nc.tensor.matmul_mx(
+                out=result[:],
+                lhsT=weight_codes[:].bitcast(FP8X4),
+                lhsT_scale=weight_scales[:],
+                rhs=codes[:].bitcast(FP8X4),
+                rhs_scale=scales[:],
+                start=True,
+                stop=True,
+            )
+            staged = first[:, c * CHUNK : (c + 1) * CHUNK] if c < CHUNKS - 1 else last[:]
+            nc.scalar.copy(staged, result[:])
+
+        scale_chunk(0)
+        for c in range(1, CHUNKS):
+            scale_chunk(c)
+            finish_chunk(c - 1)
+        nc.sync.dma_start(out[:, 0 : 3 * CHUNK], first[:])
+        finish_chunk(CHUNKS - 1)
+        nc.sync.dma_start(out[:, 3 * CHUNK : HIDDEN], last[:])

@@ -42,9 +42,9 @@ def tile_attend_lrgained_bygroup_kernel(tc, query, keys_words, keys_scales, shar
         def interleave(copy, dst, src):
             copy(dst.rearrange("p (c i) j -> p c j i", i=4), src.rearrange("p j (c i) -> p c j i", i=4))
 
-        def quantise(name, grouped, width, tag=""):
+        def quantise(name, grouped, width, tag="", plane_tag=""):
             codes = tile(name + "_codes", [P, width], U32, tag)
-            scales = tile(name + "_scales", [P, width], U8)
+            scales = tile(name + "_scales", [P, width], U8, plane_tag)
             nc.vector.quantize_mx(out=codes[:].bitcast(FP8X4), scales=scales[:], in_=grouped.rearrange("p c j -> p (c j)"))
             return codes, scales
 
@@ -53,32 +53,32 @@ def tile_attend_lrgained_bygroup_kernel(tc, query, keys_words, keys_scales, shar
                 queue.dma_start(plane[32 * quad : 32 * quad + 4, :].bitcast(I32), source[0, 4 * quad : 4 * quad + 4, :].bitcast(I32))
 
         offsets = lists.tile([P, SLOTS // 16], U16, name="offsets")
-        key_plane = tile("key_plane", [P, TOKENS], U8)
+        key_plane = tile("key_plane", [P, TOKENS], U8, "j")
         nc.vector.memset(key_plane[:].bitcast(I32), 0)
-        gain_cols = tile("gain_cols", [P, PACK], F32, "d")
-        vs_cols = tile("vs_cols", [P, PACK], F32)
-        key_pool = tile("key_pool", [P, TOKENS], U32, "k")
-        query_raw = tile("query_raw", [P, PACK, QUERIES], F32)
+        gain_cols = tile("gain_cols", [P, PACK], F32)
+        vs_cols = tile("vs_cols", [P, PACK], F32, "m")
+        key_pool = tile("key_pool", [P, TOKENS], U32)
         nc.sync.dma_start(offsets[:], offs)
-        nc.scalar.dma_start(gain_cols[:], gain.rearrange("(n c) o -> n (c o)", c=PACK))
-        nc.sync.dma_start(query_raw[:], query.rearrange("(p j) q -> p j q", j=PACK))
-        nc.scalar.dma_start(vs_cols[:], slot_scale.rearrange("o (p t) -> (o p) t", t=PACK))
+        nc.sync.dma_start(gain_cols[:], gain.rearrange("(n c) o -> n (c o)", c=PACK))
+        nc.sync.dma_start(vs_cols[:], slot_scale.rearrange("o (p t) -> (o p) t", t=PACK))
         nc.sync.dma_start(key_pool[:].bitcast(I32), keys_words[0].rearrange("p n t -> p (n t)").bitcast(I32))
         load_scale_rows(nc.scalar, key_plane, keys_scales)
 
         identity = tile("identity", [P, P], F32)
         ones = tile("ones", [P, P], F32, "a")
-        steps = tile("steps", [P, P], F32, "e")
+        steps = tile("steps", [P, P], F32, "l")
+        first_step = tile("first_step", [P, 1], F32, "e")
         ramp = tile("ramp", [P, P], F32, "c")
         in_quad = tile("in_quad", [P, 32], F32, "f")
-        quad_base = tile("quad_base", [P, 1], F32, "b")
+        quad_base = tile("quad_base", [P, 1], F32)
         warm = tile("warm", [P, 8], F32)
         nc.vector.memset(ones[:], 1.0)
         nc.vector.memset(steps[:], 1.0)
+        nc.vector.memset(first_step[:], -1.0)
         nc.vector.memset(warm[:], 0.0)
         for quad in range(4):
             nc.vector.memset(quad_base[32 * quad : 32 * quad + 32, :], 32.0 * quad)
-        nc.vector.tensor_tensor_scan(ramp[:], ones[:], steps[:], -1.0, ALU.mult, ALU.add)
+        nc.vector.tensor_tensor_scan(ramp[:], ones[:], steps[:], first_step[:], ALU.mult, ALU.add)
         nc.vector.transpose(in_quad[:], ramp[:, 0:32])
         nc.vector.tensor_scalar(identity[:], ramp[:], quad_base[:], in_quad[:, 0:1], ALU.subtract, ALU.is_equal)
         warm_out = tile("warm_out", [P, 8], F32)
@@ -89,21 +89,20 @@ def tile_attend_lrgained_bygroup_kernel(tc, query, keys_words, keys_scales, shar
             nc.sync.dma_start(raw[:], w1[:, u * 2 * CHUNK : (u + 1) * 2 * CHUNK].rearrange("(p j) r -> p j r", j=PACK))
             return raw
 
-        sharp_col = tile("sharp_col", [P, 1], F32, "a")
+        query_raw = tile("query_raw", [P, PACK, QUERIES], F32, "a")
+        sharp_col = tile("sharp_col", [P, 1], F32, "l")
         tab_pool = tile("tab_pool", [P, TOKENS], U32, "e")
-        os_cols = tile("os_cols", [P, PACK], F32, "b")
         tab_plane = tile("tab_plane", [P, TOKENS], U8, "c")
         nc.vector.memset(tab_plane[:].bitcast(I32), 0)
+        nc.sync.dma_start(query_raw[:], query.rearrange("(p j) q -> p j q", j=PACK))
         nc.sync.dma_start(sharp_col[:], sharp)
         nc.sync.dma_start(tab_pool[:].bitcast(I32), tab_words[0].rearrange("p n t -> p (n t)").bitcast(I32))
-        nc.sync.dma_start(os_cols[:], slot_factor.rearrange("o (p t) -> (o p) t", t=PACK))
         w1_raw = [load_w1(0, "f")]
         load_scale_rows(nc.scalar, tab_plane, tab_scales)
 
         gain_rows = bank(0)
         for c in range(PACK):
             nc.tensor.transpose(gain_rows[:, c, :], gain_cols[:, c : c + 1].to_broadcast([P, P]), identity[:])
-        w1_raw.append(load_w1(1, "d"))
         factor = tile("factor", [P, PACK, HIDDEN], F32)
         for t in range(PACK):
             nc.scalar.activation(
@@ -113,18 +112,21 @@ def tile_attend_lrgained_bygroup_kernel(tc, query, keys_words, keys_scales, shar
                 scale=vs_cols[:, t : t + 1],
             )
 
-        query_grouped = tile("query_grouped", [P, QUERIES, PACK], BF16)
-        interleave(nc.vector.tensor_copy, query_grouped[:], query_raw[:])
-        query_codes, query_scales = quantise("query", query_grouped[:], QUERIES)
-
         key_scales = tile("key_scales", [P, SLOTS], U8)
-        key_words = tile("key_words", [P, SLOTS], U32)
         nc.vector.tensor_copy(key_scales[:], key_plane[:].indirect(offsets[:]))
-        nc.vector.tensor_copy(key_words[:], key_pool[:].indirect(offsets[:]))
-        tab_scales_listed = tile("tab_scales_listed", [P, SLOTS], U8, "k")
+        late = tile("late", [P, PACK * 2 * CHUNK + 16], F32, "j")
+        os_cols = late[:, PACK * 2 * CHUNK : PACK * 2 * CHUNK + PACK]
+        nc.sync.dma_start(os_cols, slot_factor.rearrange("o (p t) -> (o p) t", t=PACK))
+        w1_raw.append(late[:, 0 : PACK * 2 * CHUNK].rearrange("p (j r) -> p j r", j=PACK))
+        nc.sync.dma_start(w1_raw[1], w1[:, 2 * CHUNK : 4 * CHUNK].rearrange("(p j) r -> p j r", j=PACK))
+
+        tab_scales_listed = tile("tab_scales_listed", [P, SLOTS], U8)
         nc.vector.tensor_copy(tab_scales_listed[:], tab_plane[:].indirect(offsets[:]))
-        tab_dealt = tile("tab_dealt", [P, SLOTS], U32)
-        nc.vector.tensor_copy(tab_dealt[:].rearrange("p (t s) -> p s t", t=PACK), tab_pool[:].indirect(offsets[:]))
+        key_words = tile("key_words", [P, SLOTS], U32, "c")
+        nc.vector.tensor_copy(key_words[:], key_pool[:].indirect(offsets[:]))
+        query_grouped = tile("query_grouped", [P, QUERIES, PACK], BF16, "m")
+        interleave(nc.scalar.copy, query_grouped[:], query_raw[:])
+        query_codes, query_scales = quantise("query", query_grouped[:], QUERIES)
         tab_scales_dealt = tile("tab_scales_dealt", [P, SLOTS], U8)
         nc.vector.tensor_copy(
             tab_scales_dealt[:].rearrange("p (t s) -> p t s", t=PACK),
@@ -134,35 +136,58 @@ def tile_attend_lrgained_bygroup_kernel(tc, query, keys_words, keys_scales, shar
         neg_sharp = tile("neg_sharp", [P, 1], F32)
         nc.scalar.mul(neg_sharp[:], sharp_col[:], -1.0 / GROUP)
 
-        scores = ps.tile([P, SLOTS], F32, name="bank1")
-        nc.tensor.matmul_mx(
-            out=scores[:],
-            lhsT=query_codes[:].bitcast(FP8X4),
-            lhsT_scale=query_scales[:],
-            rhs=key_words[:].bitcast(FP8X4),
-            rhs_scale=key_scales[:],
-            start=True,
-            stop=True,
-        )
-        both = tile("both", [P, PACK, 2 * P], F32)
-        nc.scalar.activation(both[:, :, 0:P], scores[:].rearrange("q (s t) -> q t s", t=PACK), ACT.Exp)
-        nc.scalar.copy(both[:, :, P : 2 * P], scores[:].rearrange("q (s t) -> q t s", t=PACK))
-
-        probs_turned = bank(2)
-        for t in range(PACK):
-            nc.tensor.transpose(probs_turned[:, t, :], both[:, t, 0:P], identity[:])
-        sums_turned = ps.tile([P, QUERIES], F32, name="bank3")
-        for j in range(GROUP):
-            nc.tensor.matmul(
-                sums_turned[:], both[:, j // 2, j % 2 : 2 * P : 2], identity[:], start=(j == 0), stop=(j == GROUP - 1), is_transpose=True
+        half = SLOTS // 2
+        probs = tile("probs", [P, PACK, P], F32)
+        score_sums = tile("score_sums", [P, GROUPS], F32)
+        score_banks = []
+        for h in range(2):
+            scores = ps.tile([P, half], F32, name="bank%d" % (1 + h))
+            nc.tensor.matmul_mx(
+                out=scores[:],
+                lhsT=query_codes[:].bitcast(FP8X4),
+                lhsT_scale=query_scales[:],
+                rhs=key_words[:, h * half : (h + 1) * half].bitcast(FP8X4),
+                rhs_scale=key_scales[:, h * half : (h + 1) * half],
+                start=True,
+                stop=True,
             )
-        weighted = tile("weighted", [P, PACK, QUERIES], F32, "h")
+            score_banks.append(scores)
+
+        def exp_half(h):
+            nc.scalar.activation(
+                probs[:, :, h * 64 : (h + 1) * 64], score_banks[h][:].rearrange("q (s t) -> q t s", t=PACK), ACT.Exp
+            )
+
+        def sum_half(h):
+            nc.vector.tensor_reduce(
+                score_sums[:, h * 32 : (h + 1) * 32], score_banks[h][:].rearrange("q (g j) -> q g j", j=GROUP), AXIS.X, ALU.add
+            )
+
+        sum_half(0)
+        exp_half(1)
+        sum_half(1)
+        exp_half(0)
+
+        neg_means = tile("neg_means", [P, GROUPS], F32, "g0")
+        neg_max = tile("neg_max", [P, 1], F32)
+        nc.vector.tensor_scalar(neg_means[:], score_sums[:], neg_sharp[:], None, ALU.mult, ALU.min, accum_out=neg_max[:])
+        group_probs = tile("group_probs", [P, GROUPS], F32)
+        group_total = tile("group_total", [P, 1], F32)
+        nc.scalar.activation(group_probs[:], neg_means[:], ACT.Exp, bias=neg_max[:], scale=-1.0, accum_out=group_total[:])
+
+        tab_dealt = tile("tab_dealt", [P, SLOTS], U32, "m")
+        nc.vector.tensor_copy(tab_dealt[:].rearrange("p (t s) -> p s t", t=PACK), tab_pool[:].indirect(offsets[:]))
+
+        probs_turned = bank(3)
+        for t in range(PACK):
+            nc.tensor.transpose(probs_turned[:, t, :], probs[:, t, :], identity[:])
+        weighted = tile("weighted", [P, PACK, QUERIES], F32)
         for t in range(PACK):
             nc.scalar.activation(weighted[:, t, :], probs_turned[:, t, :], ACT.Copy, scale=os_cols[:, t : t + 1])
-        sums_staged = tile("sums_staged", [P, QUERIES], F32)
-        nc.scalar.copy(sums_staged[:], sums_turned[:])
-        sums = ps.tile([P, 2 * GROUPS], F32, name="bank4")
-        nc.tensor.transpose(sums[:], sums_staged[:], identity[:])
+        prob_sums = tile("prob_sums", [P, GROUPS], F32, "e")
+        nc.vector.tensor_reduce(prob_sums[:], probs[:].rearrange("q t (g h) -> q g t h", h=2), AXIS.XY, ALU.add)
+        inv_sums = tile("inv_sums", [P, GROUPS], F32, "n")
+        nc.vector.reciprocal(inv_sums[:], prob_sums[:])
 
         w1_quantised = []
 
@@ -170,9 +195,8 @@ def tile_attend_lrgained_bygroup_kernel(tc, query, keys_words, keys_scales, shar
             grouped = tile("w1_grouped%d" % u, [P, 2 * CHUNK, PACK], BF16, "g%d" % u)
             for c in range(2):
                 cols = slice(c * CHUNK, (c + 1) * CHUNK)
-                copy = nc.vector.tensor_copy if (u, c) == (0, 0) else nc.scalar.copy
-                interleave(copy, grouped[:, cols, :], w1_raw[u][:, :, cols])
-            w1_quantised.append(quantise("w1_%d" % u, grouped[:], 2 * CHUNK, "e" if u == 0 else ""))
+                interleave(nc.scalar.copy, grouped[:, cols, :], w1_raw[u][:, :, cols])
+            w1_quantised.append(quantise("w1_%d" % u, grouped[:], 2 * CHUNK, "", "n" if u == 0 else ""))
 
         layer_banks = [6, 7, 0, 1]
         out_banks = [2, 3, 4, 5]
@@ -193,23 +217,9 @@ def tile_attend_lrgained_bygroup_kernel(tc, query, keys_words, keys_scales, shar
                     start=True,
                     stop=True,
                 )
-            squashed = tile("squashed%d" % c, [P, CHUNK, PACK], F32)
+            squashed = tile("squashed%d" % c, [P, CHUNK, PACK], F32, "j" if c == 0 else "")
             nc.scalar.activation(squashed[:], layer[:].rearrange("p t r -> p r t"), ACT.Tanh)
             tanhs.append(squashed)
-
-        prepare_w1(0)
-        stats = tile("stats", [P, 2, GROUPS], F32, "g0")
-        neg_means = stats[:, 0, :]
-        inv_sums = stats[:, 1, :]
-        neg_max = tile("neg_max", [P, 1], F32)
-        nc.vector.tensor_scalar(neg_means, sums[:, GROUPS : 2 * GROUPS], neg_sharp[:], None, ALU.mult, ALU.min, accum_out=neg_max[:])
-        nc.vector.reciprocal(inv_sums, sums[:, 0:GROUPS])
-        group_probs = tile("group_probs", [P, GROUPS], F32)
-        group_total = tile("group_total", [P, 1], F32)
-        nc.scalar.activation(group_probs[:], neg_means, ACT.Exp, bias=neg_max[:], scale=-1.0, accum_out=group_total[:])
-
-        prepare_w1(1)
-        layer_chunk(0)
 
         inv_total = tile("inv_total", [P, 1], F32)
         nc.vector.reciprocal(inv_total[:], group_total[:])
@@ -218,14 +228,16 @@ def tile_attend_lrgained_bygroup_kernel(tc, query, keys_words, keys_scales, shar
             shares[:],
             group_probs[:].unsqueeze(2).to_broadcast([P, GROUPS, 2]),
             inv_total[:],
-            inv_sums.unsqueeze(2).to_broadcast([P, GROUPS, 2]),
+            inv_sums[:].unsqueeze(2).to_broadcast([P, GROUPS, 2]),
             ALU.mult,
             ALU.mult,
         )
-        shares_turned = ps.tile([P, QUERIES], F32, name="bank6")
+        shares_turned = ps.tile([P, QUERIES], F32, name="bank5")
         nc.tensor.transpose(shares_turned[:], shares[:].rearrange("q g h -> q (g h)"), identity[:])
 
-        for c in range(1, CHUNKS):
+        prepare_w1(0)
+        prepare_w1(1)
+        for c in range(CHUNKS):
             layer_chunk(c)
 
         weights = tile("weights", [P, QUERIES, PACK], BF16, "i")
@@ -242,7 +254,7 @@ def tile_attend_lrgained_bygroup_kernel(tc, query, keys_words, keys_scales, shar
         scaled = []
 
         def scale_chunk(c):
-            values = tile("values%d" % c, [P, CHUNK, PACK], BF16, {2: "h", 3: "i"}.get(c, ""))
+            values = tile("values%d" % c, [P, CHUNK, PACK], BF16, {3: "i"}.get(c, ""))
             nc.vector.tensor_tensor(
                 values[:], tanhs[c][:], factor[:, :, c * CHUNK : (c + 1) * CHUNK].rearrange("p t r -> p r t"), ALU.mult
             )

@@ -31,10 +31,14 @@ def tile_attend_lrgained_bygroup_kernel(tc, query, keys_words, keys_scales, shar
     with ExitStack() as ctx:
         lists = ctx.enter_context(tc.tile_pool(name="lists", bufs=1))
         sb = ctx.enter_context(tc.tile_pool(name="sb", bufs=1))
+        placed = ctx.enter_context(tc.tile_pool(name="placed", bufs=1))
         ps = ctx.enter_context(tc.psum_pool(name="ps", bufs=1))
 
         def tile(name, shape, dtype, tag=""):
             return sb.tile(shape, dtype, name=name, tag=tag, align_bytes=64)
+
+        def tile_at(name, shape, dtype, offset):
+            return placed.tile(shape, dtype, name=name, offset=offset, align_bytes=64)
 
         def bank(index):
             return ps.tile([P, PACK, P], F32, name="bank%d" % index)
@@ -48,57 +52,49 @@ def tile_attend_lrgained_bygroup_kernel(tc, query, keys_words, keys_scales, shar
             nc.vector.quantize_mx(out=codes[:].bitcast(FP8X4), scales=scales[:], in_=grouped.rearrange("p c j -> p (c j)"))
             return codes, scales
 
-        def load_scale_rows(queue, plane, source):
+        def load_scale_rows(queues, plane, source):
             for quad in range(4):
-                queue.dma_start(plane[32 * quad : 32 * quad + 4, :].bitcast(I32), source[0, 4 * quad : 4 * quad + 4, :].bitcast(I32))
+                queues[quad % len(queues)].dma_start(plane[32 * quad : 32 * quad + 4, :].bitcast(I32), source[0, 4 * quad : 4 * quad + 4, :].bitcast(I32))
 
         offsets = lists.tile([P, SLOTS // 16], U16, name="offsets")
-        key_plane = tile("key_plane", [P, TOKENS], U8, "j")
+        key_plane = tile("key_plane", [P, TOKENS], U8)
         nc.vector.memset(key_plane[:].bitcast(I32), 0)
         gain_cols = tile("gain_cols", [P, PACK], F32)
         vs_cols = tile("vs_cols", [P, PACK], F32, "m")
-        key_pool = tile("key_pool", [P, TOKENS], U32)
+        key_pool = tile_at("key_pool", [P, TOKENS], U32, 0)
+        query_raw = tile("query_raw", [P, PACK, QUERIES], F32)
         nc.sync.dma_start(offsets[:], offs)
-        nc.sync.dma_start(gain_cols[:], gain.rearrange("(n c) o -> n (c o)", c=PACK))
-        nc.sync.dma_start(vs_cols[:], slot_scale.rearrange("o (p t) -> (o p) t", t=PACK))
         nc.sync.dma_start(key_pool[:].bitcast(I32), keys_words[0].rearrange("p n t -> p (n t)").bitcast(I32))
-        load_scale_rows(nc.scalar, key_plane, keys_scales)
+        nc.sync.dma_start(query_raw[:], query.rearrange("(p j) q -> p j q", j=PACK))
+        nc.scalar.dma_start(gain_cols[:], gain.rearrange("(n c) o -> n (c o)", c=PACK))
+        nc.scalar.dma_start(vs_cols[:], slot_scale.rearrange("o (p t) -> (o p) t", t=PACK))
+        load_scale_rows([nc.sync], key_plane, keys_scales)
 
         identity = tile("identity", [P, P], F32)
-        ones = tile("ones", [P, P], F32, "a")
-        steps = tile("steps", [P, P], F32, "l")
-        first_step = tile("first_step", [P, 1], F32, "e")
-        ramp = tile("ramp", [P, P], F32, "c")
-        in_quad = tile("in_quad", [P, 32], F32, "f")
-        quad_base = tile("quad_base", [P, 1], F32)
-        warm = tile("warm", [P, 8], F32)
+        ones = tile("ones", [P, P], F32)
+        ramp = tile_at("ramp", [P, P], F32, 16640)
+        in_quad = tile("in_quad", [P, 32], F32, "e")
+        quad_base = tile("quad_base", [P, 1], F32, "l")
+        zero = tile("zero", [P, 1], F32)
         nc.vector.memset(ones[:], 1.0)
-        nc.vector.memset(steps[:], 1.0)
-        nc.vector.memset(first_step[:], -1.0)
-        nc.vector.memset(warm[:], 0.0)
+        nc.vector.memset(zero[:], 0.0)
         for quad in range(4):
             nc.vector.memset(quad_base[32 * quad : 32 * quad + 32, :], 32.0 * quad)
-        nc.vector.tensor_tensor_scan(ramp[:], ones[:], steps[:], first_step[:], ALU.mult, ALU.add)
+        nc.vector.tensor_tensor_scan(ramp[:], ones[:], ones[:], -1.0, ALU.mult, ALU.add)
         nc.vector.transpose(in_quad[:], ramp[:, 0:32])
         nc.vector.tensor_scalar(identity[:], ramp[:], quad_base[:], in_quad[:, 0:1], ALU.subtract, ALU.is_equal)
-        warm_out = tile("warm_out", [P, 8], F32)
-        nc.scalar.activation(warm_out[:], warm[:], ACT.Exp)
+        warm_out = tile("warm_out", [P, 1], F32)
+        nc.scalar.activation(warm_out[:], zero[:], ACT.Exp)
 
-        def load_w1(u, tag):
-            raw = tile("w1_raw%d" % u, [P, PACK, 2 * CHUNK], F32, tag)
-            nc.sync.dma_start(raw[:], w1[:, u * 2 * CHUNK : (u + 1) * 2 * CHUNK].rearrange("(p j) r -> p j r", j=PACK))
-            return raw
-
-        query_raw = tile("query_raw", [P, PACK, QUERIES], F32, "a")
+        tab_pool = tile_at("tab_pool", [P, TOKENS], U32, 8704)
         sharp_col = tile("sharp_col", [P, 1], F32, "l")
-        tab_pool = tile("tab_pool", [P, TOKENS], U32, "e")
-        tab_plane = tile("tab_plane", [P, TOKENS], U8, "c")
-        nc.vector.memset(tab_plane[:].bitcast(I32), 0)
-        nc.sync.dma_start(query_raw[:], query.rearrange("(p j) q -> p j q", j=PACK))
-        nc.sync.dma_start(sharp_col[:], sharp)
+        os_cols = tile("os_cols", [P, PACK], F32, "e")
+        tab_plane = tile_at("tab_plane", [P, TOKENS], U8, 16896)
         nc.sync.dma_start(tab_pool[:].bitcast(I32), tab_words[0].rearrange("p n t -> p (n t)").bitcast(I32))
-        w1_raw = [load_w1(0, "f")]
-        load_scale_rows(nc.scalar, tab_plane, tab_scales)
+        nc.sync.dma_start(sharp_col[:], sharp)
+        nc.sync.dma_start(os_cols[:], slot_factor.rearrange("o (p t) -> (o p) t", t=PACK))
+        nc.vector.memset(tab_plane[:].bitcast(I32), 0)
+        load_scale_rows([nc.sync], tab_plane, tab_scales)
 
         gain_rows = bank(0)
         for c in range(PACK):
@@ -112,32 +108,25 @@ def tile_attend_lrgained_bygroup_kernel(tc, query, keys_words, keys_scales, shar
                 scale=vs_cols[:, t : t + 1],
             )
 
-        key_scales = tile("key_scales", [P, SLOTS], U8)
-        nc.vector.tensor_copy(key_scales[:], key_plane[:].indirect(offsets[:]))
-        late = tile("late", [P, PACK * 2 * CHUNK + 16], F32, "j")
-        os_cols = late[:, PACK * 2 * CHUNK : PACK * 2 * CHUNK + PACK]
-        nc.sync.dma_start(os_cols, slot_factor.rearrange("o (p t) -> (o p) t", t=PACK))
-        w1_raw.append(late[:, 0 : PACK * 2 * CHUNK].rearrange("p (j r) -> p j r", j=PACK))
-        nc.sync.dma_start(w1_raw[1], w1[:, 2 * CHUNK : 4 * CHUNK].rearrange("(p j) r -> p j r", j=PACK))
-
-        tab_scales_listed = tile("tab_scales_listed", [P, SLOTS], U8)
-        nc.vector.tensor_copy(tab_scales_listed[:], tab_plane[:].indirect(offsets[:]))
-        key_words = tile("key_words", [P, SLOTS], U32, "c")
+        key_words = tile("key_words", [P, SLOTS], U32)
         nc.vector.tensor_copy(key_words[:], key_pool[:].indirect(offsets[:]))
+        key_scales = tile_at("key_scales", [P, SLOTS], U8, 0)
+        nc.vector.tensor_copy(key_scales[:], key_plane[:].indirect(offsets[:]))
+        w1_raw = [tile_at("w1_raw%d" % u, [P, PACK, 2 * CHUNK], F32, 512 + 4096 * u) for u in range(2)]
+        for u in range(2):
+            nc.sync.dma_start(w1_raw[u][:], w1[:, u * 2 * CHUNK : (u + 1) * 2 * CHUNK].rearrange("(p j) r -> p j r", j=PACK))
+
         query_grouped = tile("query_grouped", [P, QUERIES, PACK], BF16, "m")
         interleave(nc.scalar.copy, query_grouped[:], query_raw[:])
         query_codes, query_scales = quantise("query", query_grouped[:], QUERIES)
-        tab_scales_dealt = tile("tab_scales_dealt", [P, SLOTS], U8)
-        nc.vector.tensor_copy(
-            tab_scales_dealt[:].rearrange("p (t s) -> p t s", t=PACK),
-            tab_scales_listed[:].rearrange("p (s t) -> p t s", t=PACK),
-        )
+        tab_dealt = tile("tab_dealt", [P, SLOTS], U32, "m")
+        nc.vector.tensor_copy(tab_dealt[:].rearrange("p (t s) -> p s t", t=PACK), tab_pool[:].indirect(offsets[:]))
 
         neg_sharp = tile("neg_sharp", [P, 1], F32)
         nc.scalar.mul(neg_sharp[:], sharp_col[:], -1.0 / GROUP)
 
         half = SLOTS // 2
-        probs = tile("probs", [P, PACK, P], F32)
+        probs = tile("probs", [P, PACK, P], F32, "i")
         score_sums = tile("score_sums", [P, GROUPS], F32)
         score_banks = []
         for h in range(2):
@@ -163,20 +152,10 @@ def tile_attend_lrgained_bygroup_kernel(tc, query, keys_words, keys_scales, shar
                 score_sums[:, h * 32 : (h + 1) * 32], score_banks[h][:].rearrange("q (g j) -> q g j", j=GROUP), AXIS.X, ALU.add
             )
 
-        sum_half(0)
-        exp_half(1)
-        sum_half(1)
         exp_half(0)
-
-        neg_means = tile("neg_means", [P, GROUPS], F32, "g0")
-        neg_max = tile("neg_max", [P, 1], F32)
-        nc.vector.tensor_scalar(neg_means[:], score_sums[:], neg_sharp[:], None, ALU.mult, ALU.min, accum_out=neg_max[:])
-        group_probs = tile("group_probs", [P, GROUPS], F32)
-        group_total = tile("group_total", [P, 1], F32)
-        nc.scalar.activation(group_probs[:], neg_means[:], ACT.Exp, bias=neg_max[:], scale=-1.0, accum_out=group_total[:])
-
-        tab_dealt = tile("tab_dealt", [P, SLOTS], U32, "m")
-        nc.vector.tensor_copy(tab_dealt[:].rearrange("p (t s) -> p s t", t=PACK), tab_pool[:].indirect(offsets[:]))
+        exp_half(1)
+        sum_half(0)
+        sum_half(1)
 
         probs_turned = bank(3)
         for t in range(PACK):
@@ -184,19 +163,31 @@ def tile_attend_lrgained_bygroup_kernel(tc, query, keys_words, keys_scales, shar
         weighted = tile("weighted", [P, PACK, QUERIES], F32)
         for t in range(PACK):
             nc.scalar.activation(weighted[:, t, :], probs_turned[:, t, :], ACT.Copy, scale=os_cols[:, t : t + 1])
-        prob_sums = tile("prob_sums", [P, GROUPS], F32, "e")
+
+        neg_means = tile("neg_means", [P, GROUPS], F32)
+        neg_max = tile("neg_max", [P, 1], F32, "n")
+        nc.vector.tensor_scalar(neg_means[:], score_sums[:], neg_sharp[:], None, ALU.mult, ALU.min, accum_out=neg_max[:])
+
+        tab_scales_listed = tile_at("tab_scales_listed", [P, SLOTS], U8, 8704)
+        nc.vector.tensor_copy(tab_scales_listed[:], tab_plane[:].indirect(offsets[:]))
+        tab_scales_dealt = tile("tab_scales_dealt", [P, SLOTS], U8)
+        nc.vector.tensor_copy(
+            tab_scales_dealt[:].rearrange("p (t s) -> p t s", t=PACK),
+            tab_scales_listed[:].rearrange("p (s t) -> p t s", t=PACK),
+        )
+        prob_sums = tile("prob_sums", [P, GROUPS], F32)
         nc.vector.tensor_reduce(prob_sums[:], probs[:].rearrange("q t (g h) -> q g t h", h=2), AXIS.XY, ALU.add)
-        inv_sums = tile("inv_sums", [P, GROUPS], F32, "n")
+        inv_sums = tile("inv_sums", [P, GROUPS], F32)
         nc.vector.reciprocal(inv_sums[:], prob_sums[:])
 
         w1_quantised = []
 
         def prepare_w1(u):
-            grouped = tile("w1_grouped%d" % u, [P, 2 * CHUNK, PACK], BF16, "g%d" % u)
+            grouped = tile("w1_grouped%d" % u, [P, 2 * CHUNK, PACK], BF16, "en"[u])
             for c in range(2):
                 cols = slice(c * CHUNK, (c + 1) * CHUNK)
                 interleave(nc.scalar.copy, grouped[:, cols, :], w1_raw[u][:, :, cols])
-            w1_quantised.append(quantise("w1_%d" % u, grouped[:], 2 * CHUNK, "", "n" if u == 0 else ""))
+            w1_quantised.append(quantise("w1_%d" % u, grouped[:], 2 * CHUNK, "", "i" if u == 0 else ""))
 
         layer_banks = [6, 7, 0, 1]
         out_banks = [2, 3, 4, 5]
@@ -217,13 +208,17 @@ def tile_attend_lrgained_bygroup_kernel(tc, query, keys_words, keys_scales, shar
                     start=True,
                     stop=True,
                 )
-            squashed = tile("squashed%d" % c, [P, CHUNK, PACK], F32, "j" if c == 0 else "")
+            squashed = tile_at("squashed0", [P, CHUNK, PACK], F32, 4608) if c == 0 else tile("squashed%d" % c, [P, CHUNK, PACK], F32)
             nc.scalar.activation(squashed[:], layer[:].rearrange("p t r -> p r t"), ACT.Tanh)
             tanhs.append(squashed)
 
+        prepare_w1(0)
+        group_probs = tile_at("group_probs", [P, GROUPS], F32, 512)
+        group_total = tile("group_total", [P, 1], F32)
+        nc.scalar.activation(group_probs[:], neg_means[:], ACT.Exp, bias=neg_max[:], scale=-1.0, accum_out=group_total[:])
         inv_total = tile("inv_total", [P, 1], F32)
         nc.vector.reciprocal(inv_total[:], group_total[:])
-        shares = tile("shares", [P, GROUPS, 2], F32)
+        shares = tile("shares", [P, GROUPS, 2], F32, "e")
         nc.vector.scalar_tensor_tensor(
             shares[:],
             group_probs[:].unsqueeze(2).to_broadcast([P, GROUPS, 2]),
@@ -235,12 +230,8 @@ def tile_attend_lrgained_bygroup_kernel(tc, query, keys_words, keys_scales, shar
         shares_turned = ps.tile([P, QUERIES], F32, name="bank5")
         nc.tensor.transpose(shares_turned[:], shares[:].rearrange("q g h -> q (g h)"), identity[:])
 
-        prepare_w1(0)
         prepare_w1(1)
-        for c in range(CHUNKS):
-            layer_chunk(c)
-
-        weights = tile("weights", [P, QUERIES, PACK], BF16, "i")
+        weights = tile("weights", [P, QUERIES, PACK], BF16, "n")
         nc.vector.tensor_tensor(
             weights[:],
             weighted[:].rearrange("p t q -> p q t"),
@@ -249,12 +240,15 @@ def tile_attend_lrgained_bygroup_kernel(tc, query, keys_words, keys_scales, shar
         )
         weight_codes, weight_scales = quantise("weights", weights[:], QUERIES)
 
+        for c in range(CHUNKS):
+            layer_chunk(c)
+
         first = tile("first", [P, 3 * CHUNK], F32)
         last = tile("last", [P, CHUNK], F32)
         scaled = []
 
         def scale_chunk(c):
-            values = tile("values%d" % c, [P, CHUNK, PACK], BF16, {3: "i"}.get(c, ""))
+            values = tile("values%d" % c, [P, CHUNK, PACK], BF16)
             nc.vector.tensor_tensor(
                 values[:], tanhs[c][:], factor[:, :, c * CHUNK : (c + 1) * CHUNK].rearrange("p t r -> p r t"), ALU.mult
             )

@@ -62,25 +62,25 @@ def tile_attend_lrgained_bygroup_kernel(tc, query, keys_words, keys_scales, shar
         gain_cols = tile("gain_cols", [P, PACK], F32)
         vs_cols = tile("vs_cols", [P, PACK], F32, "m")
         key_pool = tile_at("key_pool", [P, TOKENS], U32, 0)
-        query_raw = tile("query_raw", [P, PACK, QUERIES], F32)
         nc.sync.dma_start(offsets[:], offs)
         nc.sync.dma_start(key_pool[:].bitcast(I32), keys_words[0].rearrange("p n t -> p (n t)").bitcast(I32))
-        nc.sync.dma_start(query_raw[:], query.rearrange("(p j) q -> p j q", j=PACK))
         nc.scalar.dma_start(gain_cols[:], gain.rearrange("(n c) o -> n (c o)", c=PACK))
         nc.scalar.dma_start(vs_cols[:], slot_scale.rearrange("o (p t) -> (o p) t", t=PACK))
-        load_scale_rows([nc.sync], key_plane, keys_scales)
+        load_scale_rows([nc.scalar], key_plane, keys_scales)
 
         identity = tile("identity", [P, P], F32)
-        ones = tile("ones", [P, P], F32)
+        ones = tile_at("ones", [P, P], F32, 18944)
         ramp = tile_at("ramp", [P, P], F32, 16640)
         in_quad = tile("in_quad", [P, 32], F32, "e")
         quad_base = tile("quad_base", [P, 1], F32, "l")
-        zero = tile("zero", [P, 1], F32)
         nc.vector.memset(ones[:], 1.0)
-        nc.vector.memset(zero[:], 0.0)
         for quad in range(4):
             nc.vector.memset(quad_base[32 * quad : 32 * quad + 32, :], 32.0 * quad)
         nc.vector.tensor_tensor_scan(ramp[:], ones[:], ones[:], -1.0, ALU.mult, ALU.add)
+        zero = tile_at("zero", [P, 1], F32, 18944)
+        nc.vector.memset(zero[:], 0.0)
+        query_raw = tile_at("query_raw", [P, PACK, QUERIES], F32, 19008)
+        nc.sync.dma_start(query_raw[:], query.rearrange("(p j) q -> p j q", j=PACK))
         nc.vector.transpose(in_quad[:], ramp[:, 0:32])
         nc.vector.tensor_scalar(identity[:], ramp[:], quad_base[:], in_quad[:, 0:1], ALU.subtract, ALU.is_equal)
         warm_out = tile("warm_out", [P, 1], F32)
@@ -177,7 +177,7 @@ def tile_attend_lrgained_bygroup_kernel(tc, query, keys_words, keys_scales, shar
         )
         prob_sums = tile("prob_sums", [P, GROUPS], F32)
         nc.vector.tensor_reduce(prob_sums[:], probs[:].rearrange("q t (g h) -> q g t h", h=2), AXIS.XY, ALU.add)
-        inv_sums = tile("inv_sums", [P, GROUPS], F32)
+        inv_sums = tile("inv_sums", [P, GROUPS], F32, "h")
         nc.vector.reciprocal(inv_sums[:], prob_sums[:])
 
         w1_quantised = []
@@ -186,8 +186,8 @@ def tile_attend_lrgained_bygroup_kernel(tc, query, keys_words, keys_scales, shar
             grouped = tile("w1_grouped%d" % u, [P, 2 * CHUNK, PACK], BF16, "en"[u])
             for c in range(2):
                 cols = slice(c * CHUNK, (c + 1) * CHUNK)
-                interleave(nc.scalar.copy, grouped[:, cols, :], w1_raw[u][:, :, cols])
-            w1_quantised.append(quantise("w1_%d" % u, grouped[:], 2 * CHUNK, "", "i" if u == 0 else ""))
+                interleave(nc.vector.tensor_copy if (u, c) == (1, 1) else nc.scalar.copy, grouped[:, cols, :], w1_raw[u][:, :, cols])
+            w1_quantised.append(quantise("w1_%d" % u, grouped[:], 2 * CHUNK, "", "ih"[u]))
 
         layer_banks = [6, 7, 0, 1]
         out_banks = [2, 3, 4, 5]
@@ -227,11 +227,14 @@ def tile_attend_lrgained_bygroup_kernel(tc, query, keys_words, keys_scales, shar
             ALU.mult,
             ALU.mult,
         )
+        prepare_w1(1)
+        layer_chunk(0)
+        layer_chunk(1)
         shares_turned = ps.tile([P, QUERIES], F32, name="bank5")
         nc.tensor.transpose(shares_turned[:], shares[:].rearrange("q g h -> q (g h)"), identity[:])
-
-        prepare_w1(1)
-        weights = tile("weights", [P, QUERIES, PACK], BF16, "n")
+        layer_chunk(2)
+        layer_chunk(3)
+        weights = tile("weights", [P, QUERIES, PACK], BF16)
         nc.vector.tensor_tensor(
             weights[:],
             weighted[:].rearrange("p t q -> p q t"),
@@ -239,9 +242,6 @@ def tile_attend_lrgained_bygroup_kernel(tc, query, keys_words, keys_scales, shar
             ALU.mult,
         )
         weight_codes, weight_scales = quantise("weights", weights[:], QUERIES)
-
-        for c in range(CHUNKS):
-            layer_chunk(c)
 
         first = tile("first", [P, 3 * CHUNK], F32)
         last = tile("last", [P, CHUNK], F32)

from contextlib import ExitStack

import concourse.mybir as mybir

F32 = mybir.dt.float32
BF16 = mybir.dt.bfloat16
I32 = mybir.dt.int32
U32 = mybir.dt.uint32
U16 = mybir.dt.uint16
U8 = mybir.dt.uint8
FP8X4 = mybir.dt.float8_e4m3fn_x4
ALU = mybir.AluOpType
ACT = mybir.ActivationFunctionType
AXIS = mybir.AxisListType

P = 128
PACK = 4
TOKENS = 2048
SLOTS = 512
HIDDEN = 512
QUERIES = 128
GROUP = 8
GROUPS = SLOTS // GROUP
CHUNK = 128
CHUNKS = HIDDEN // CHUNK
FLOPS = 2 * 512 * QUERIES * SLOTS + 2 * 512 * HIDDEN * SLOTS + 2 * SLOTS * QUERIES * HIDDEN


def tile_attend_lrgained_bygroup_kernel(tc, query, keys_words, keys_scales, sharp, tab_words, tab_scales, w1, gain, slot_factor, slot_scale, offs, out):
    nc = tc.nc
    with ExitStack() as ctx:
        lists = ctx.enter_context(tc.tile_pool(name="lists", bufs=1))
        sb = ctx.enter_context(tc.tile_pool(name="sb", bufs=1))
        placed = ctx.enter_context(tc.tile_pool(name="placed", bufs=1))
        ps = ctx.enter_context(tc.psum_pool(name="ps", bufs=1))

        def tile(name, shape, dtype, tag=""):
            return sb.tile(shape, dtype, name=name, tag=tag, align_bytes=64)

        def tile_at(name, shape, dtype, offset):
            return placed.tile(shape, dtype, name=name, offset=offset, align_bytes=64)

        def bank(index):
            return ps.tile([P, PACK, P], F32, name="bank%d" % index)

        def interleave(copy, dst, src):
            copy(dst.rearrange("p (c i) j -> p c j i", i=4), src.rearrange("p j (c i) -> p c j i", i=4))

        def quantise(name, grouped, width, tag="", plane_tag=""):
            codes = tile(name + "_codes", [P, width], U32, tag)
            scales = tile(name + "_scales", [P, width], U8, plane_tag)
            nc.vector.quantize_mx(out=codes[:].bitcast(FP8X4), scales=scales[:], in_=grouped.rearrange("p c j -> p (c j)"))
            return codes, scales

        def load_scale_rows(queues, plane, source):
            for quad in range(4):
                queues[quad % len(queues)].dma_start(plane[32 * quad : 32 * quad + 4, :].bitcast(I32), source[0, 4 * quad : 4 * quad + 4, :].bitcast(I32))

        offsets = lists.tile([P, SLOTS // 16], U16, name="offsets")
        key_plane = tile("key_plane", [P, TOKENS], U8)
        nc.vector.memset(key_plane[:].bitcast(I32), 0)
        gain_cols = tile("gain_cols", [P, PACK], F32)
        vs_cols = tile("vs_cols", [P, PACK], F32, "m")
        key_pool = tile_at("key_pool", [P, TOKENS], U32, 0)
        nc.sync.dma_start(offsets[:], offs)
        nc.sync.dma_start(key_pool[:].bitcast(I32), keys_words[0].rearrange("p n t -> p (n t)").bitcast(I32))
        nc.scalar.dma_start(gain_cols[:], gain.rearrange("(n c) o -> n (c o)", c=PACK))
        nc.scalar.dma_start(vs_cols[:], slot_scale.rearrange("o (p t) -> (o p) t", t=PACK))
        load_scale_rows([nc.scalar], key_plane, keys_scales)

        identity = tile("identity", [P, P], F32)
        ones = tile_at("ones", [P, P], F32, 18944)
        ramp = tile_at("ramp", [P, P], F32, 16640)
        in_quad = tile("in_quad", [P, 32], F32, "e")
        quad_base = tile("quad_base", [P, 1], F32, "l")
        nc.vector.memset(ones[:], 1.0)
        for quad in range(4):
            nc.vector.memset(quad_base[32 * quad : 32 * quad + 32, :], 32.0 * quad)
        nc.vector.tensor_tensor_scan(ramp[:], ones[:], ones[:], -1.0, ALU.mult, ALU.add)
        zero = tile_at("zero", [P, 1], F32, 18944)
        nc.vector.memset(zero[:], 0.0)
        query_raw = tile_at("query_raw", [P, PACK, QUERIES], F32, 19008)
        nc.sync.dma_start(query_raw[:], query.rearrange("(p j) q -> p j q", j=PACK))
        nc.vector.transpose(in_quad[:], ramp[:, 0:32])
        nc.vector.tensor_scalar(identity[:], ramp[:], quad_base[:], in_quad[:, 0:1], ALU.subtract, ALU.is_equal)
        warm_out = tile("warm_out", [P, 1], F32)
        nc.scalar.activation(warm_out[:], zero[:], ACT.Exp)

        tab_pool = tile_at("tab_pool", [P, TOKENS], U32, 8704)
        sharp_col = tile("sharp_col", [P, 1], F32, "l")
        os_cols = tile("os_cols", [P, PACK], F32, "e")
        tab_plane = tile_at("tab_plane", [P, TOKENS], U8, 16896)
        nc.sync.dma_start(tab_pool[:].bitcast(I32), tab_words[0].rearrange("p n t -> p (n t)").bitcast(I32))
        nc.sync.dma_start(sharp_col[:], sharp)
        nc.sync.dma_start(os_cols[:], slot_factor.rearrange("o (p t) -> (o p) t", t=PACK))
        nc.vector.memset(tab_plane[:].bitcast(I32), 0)
        load_scale_rows([nc.sync], tab_plane, tab_scales)

        gain_rows = bank(0)
        for c in range(PACK):
            nc.tensor.transpose(gain_rows[:, c, :], gain_cols[:, c : c + 1].to_broadcast([P, P]), identity[:])
        factor = tile("factor", [P, PACK, HIDDEN], F32)
        for t in range(PACK):
            nc.scalar.activation(
                factor[:, t, :].rearrange("p (n c) -> p n c", c=PACK),
                gain_rows[:].rearrange("p c n -> p n c"),
                ACT.Copy,
                scale=vs_cols[:, t : t + 1],
            )

        key_words = tile("key_words", [P, SLOTS], U32)
        nc.vector.tensor_copy(key_words[:], key_pool[:].indirect(offsets[:]))
        key_scales = tile_at("key_scales", [P, SLOTS], U8, 0)
        nc.vector.tensor_copy(key_scales[:], key_plane[:].indirect(offsets[:]))
        w1_raw = [tile_at("w1_raw%d" % u, [P, PACK, 2 * CHUNK], F32, 512 + 4096 * u) for u in range(2)]
        for u in range(2):
            nc.sync.dma_start(w1_raw[u][:], w1[:, u * 2 * CHUNK : (u + 1) * 2 * CHUNK].rearrange("(p j) r -> p j r", j=PACK))

        query_grouped = tile("query_grouped", [P, QUERIES, PACK], BF16, "m")
        interleave(nc.scalar.copy, query_grouped[:], query_raw[:])
        query_codes, query_scales = quantise("query", query_grouped[:], QUERIES)
        tab_dealt = tile("tab_dealt", [P, SLOTS], U32, "m")
        nc.vector.tensor_copy(tab_dealt[:].rearrange("p (t s) -> p s t", t=PACK), tab_pool[:].indirect(offsets[:]))

        neg_sharp = tile("neg_sharp", [P, 1], F32)
        nc.scalar.mul(neg_sharp[:], sharp_col[:], -1.0 / GROUP)

        half = SLOTS // 2
        probs = tile("probs", [P, PACK, P], F32, "i")
        score_sums = tile("score_sums", [P, GROUPS], F32)
        score_banks = []
        for h in range(2):
            scores = ps.tile([P, half], F32, name="bank%d" % (1 + h))
            nc.tensor.matmul_mx(
                out=scores[:],
                lhsT=query_codes[:].bitcast(FP8X4),
                lhsT_scale=query_scales[:],
                rhs=key_words[:, h * half : (h + 1) * half].bitcast(FP8X4),
                rhs_scale=key_scales[:, h * half : (h + 1) * half],
                start=True,
                stop=True,
            )
            score_banks.append(scores)

        def exp_half(h):
            nc.scalar.activation(
                probs[:, :, h * 64 : (h + 1) * 64], score_banks[h][:].rearrange("q (s t) -> q t s", t=PACK), ACT.Exp
            )

        def sum_half(h):
            nc.vector.tensor_reduce(
                score_sums[:, h * 32 : (h + 1) * 32], score_banks[h][:].rearrange("q (g j) -> q g j", j=GROUP), AXIS.X, ALU.add
            )

        exp_half(0)
        exp_half(1)
        sum_half(0)
        sum_half(1)

        probs_turned = bank(3)
        for t in range(PACK):
            nc.tensor.transpose(probs_turned[:, t, :], probs[:, t, :], identity[:])
        weighted = tile("weighted", [P, PACK, QUERIES], F32)
        for t in range(PACK):
            nc.scalar.activation(weighted[:, t, :], probs_turned[:, t, :], ACT.Copy, scale=os_cols[:, t : t + 1])

        neg_means = tile("neg_means", [P, GROUPS], F32)
        neg_max = tile("neg_max", [P, 1], F32, "n")
        nc.vector.tensor_scalar(neg_means[:], score_sums[:], neg_sharp[:], None, ALU.mult, ALU.min, accum_out=neg_max[:])

        tab_scales_listed = tile_at("tab_scales_listed", [P, SLOTS], U8, 8704)
        nc.vector.tensor_copy(tab_scales_listed[:], tab_plane[:].indirect(offsets[:]))
        tab_scales_dealt = tile("tab_scales_dealt", [P, SLOTS], U8)
        nc.vector.tensor_copy(
            tab_scales_dealt[:].rearrange("p (t s) -> p t s", t=PACK),
            tab_scales_listed[:].rearrange("p (s t) -> p t s", t=PACK),
        )
        prob_sums = tile("prob_sums", [P, GROUPS], F32)
        nc.vector.tensor_reduce(prob_sums[:], probs[:].rearrange("q t (g h) -> q g t h", h=2), AXIS.XY, ALU.add)
        inv_sums = tile("inv_sums", [P, GROUPS], F32, "h")
        nc.vector.reciprocal(inv_sums[:], prob_sums[:])

        w1_quantised = []

        def prepare_w1(u):
            grouped = tile("w1_grouped%d" % u, [P, 2 * CHUNK, PACK], BF16, "en"[u])
            for c in range(2):
                cols = slice(c * CHUNK, (c + 1) * CHUNK)
                interleave(nc.vector.tensor_copy if (u, c) == (1, 1) else nc.scalar.copy, grouped[:, cols, :], w1_raw[u][:, :, cols])
            w1_quantised.append(quantise("w1_%d" % u, grouped[:], 2 * CHUNK, "", "ih"[u]))

        layer_banks = [6, 7, 0, 1]
        out_banks = [2, 3, 4, 5]
        tanhs = []

        def layer_chunk(c):
            layer = bank(layer_banks[c])
            codes, scales = w1_quantised[c // 2]
            cols = slice((c % 2) * CHUNK, (c % 2 + 1) * CHUNK)
            for t in range(PACK):
                slots = slice(t * P, (t + 1) * P)
                nc.tensor.matmul_mx(
                    out=layer[:, t, :],
                    lhsT=tab_dealt[:, slots].bitcast(FP8X4),
                    lhsT_scale=tab_scales_dealt[:, slots],
                    rhs=codes[:, cols].bitcast(FP8X4),
                    rhs_scale=scales[:, cols],
                    start=True,
                    stop=True,
                )
            squashed = tile_at("squashed0", [P, CHUNK, PACK], F32, 4608) if c == 0 else tile("squashed%d" % c, [P, CHUNK, PACK], F32)
            nc.scalar.activation(squashed[:], layer[:].rearrange("p t r -> p r t"), ACT.Tanh)
            tanhs.append(squashed)

        prepare_w1(0)
        group_probs = tile_at("group_probs", [P, GROUPS], F32, 512)
        group_total = tile("group_total", [P, 1], F32)
        nc.scalar.activation(group_probs[:], neg_means[:], ACT.Exp, bias=neg_max[:], scale=-1.0, accum_out=group_total[:])
        inv_total = tile("inv_total", [P, 1], F32)
        nc.vector.reciprocal(inv_total[:], group_total[:])
        shares = tile("shares", [P, GROUPS, 2], F32, "e")
        nc.vector.scalar_tensor_tensor(
            shares[:],
            group_probs[:].unsqueeze(2).to_broadcast([P, GROUPS, 2]),
            inv_total[:],
            inv_sums[:].unsqueeze(2).to_broadcast([P, GROUPS, 2]),
            ALU.mult,
            ALU.mult,
        )
        prepare_w1(1)
        layer_chunk(0)
        layer_chunk(1)
        shares_turned = ps.tile([P, QUERIES], F32, name="bank5")
        nc.tensor.transpose(shares_turned[:], shares[:].rearrange("q g h -> q (g h)"), identity[:])
        layer_chunk(2)
        layer_chunk(3)
        weights = tile("weights", [P, QUERIES, PACK], BF16)
        nc.vector.tensor_tensor(
            weights[:],
            weighted[:].rearrange("p t q -> p q t"),
            shares_turned[:].unsqueeze(2).to_broadcast([P, QUERIES, PACK]),
            ALU.mult,
        )
        weight_codes, weight_scales = quantise("weights", weights[:], QUERIES)

        first = tile("first", [P, 3 * CHUNK], F32)
        last = tile("last", [P, CHUNK], F32)
        scaled = []

        def scale_chunk(c):
            values = tile("values%d" % c, [P, CHUNK, PACK], BF16)
            nc.vector.tensor_tensor(
                values[:], tanhs[c][:], factor[:, :, c * CHUNK : (c + 1) * CHUNK].rearrange("p t r -> p r t"), ALU.mult
            )
            scaled.append(values)

        def finish_chunk(c):
            codes, scales = quantise("values%d" % c, scaled[c][:], CHUNK)
            result = ps.tile([P, CHUNK], F32, name="bank%d" % out_banks[c])
            nc.tensor.matmul_mx(
                out=result[:],
                lhsT=weight_codes[:].bitcast(FP8X4),
                lhsT_scale=weight_scales[:],
                rhs=codes[:].bitcast(FP8X4),
                rhs_scale=scales[:],
                start=True,
                stop=True,
            )
            staged = first[:, c * CHUNK : (c + 1) * CHUNK] if c < CHUNKS - 1 else last[:]
            nc.scalar.copy(staged, result[:])

        scale_chunk(0)
        for c in range(1, CHUNKS):
            scale_chunk(c)
            finish_chunk(c - 1)
        nc.sync.dma_start(out[:, 0 : 3 * CHUNK], first[:])
        finish_chunk(CHUNKS - 1)
        nc.sync.dma_start(out[:, 3 * CHUNK : HIDDEN], last[:])
